import numpy as np, ml_dtypes
CORES = [40,41,42,43,44,45,46,47]
N = 8
import mx_ref
BF = ml_dtypes.bfloat16
def entries(a):
    return np.ascontiguousarray(a.T).reshape(-1)
def table(e):
    return np.ascontiguousarray(np.reshape(e, (-1, 16)).T).astype(np.int32)
def cut(t, i, w=512):
    return t[:, w * i:w * i + w]
def f(rng, *shape):
    return mx_ref.flush((rng.standard_normal(shape, dtype=np.float32) * np.exp2(rng.integers(-2, 3, shape[:-1] + (1,)))).astype(BF))
def wide(rng, *shape, cols=0):
    v = rng.standard_normal(shape, dtype=np.float32) * np.exp2(rng.integers(-12, 13, shape)).astype(np.float32)
    if cols: v *= np.repeat(np.exp2(rng.integers(-cols, cols + 1, shape[:-2] + (1, shape[-1] // 4))) * (rng.random(shape[:-2] + (1, shape[-1] // 4)) > 0.0625), 4, axis=-1).astype(np.float32)
    return mx_ref.flush(v.astype(BF))
T, S, CAPP, O = 512, 512, 128, 4
def counts(rng, zero=0.125, quiet=()):
    send = [r for r in range(N) if r not in quiet]
    n = np.zeros((N, N), int)
    for d in range(N): n[send[rng.integers(0, len(send))], d] = 16
    for k in rng.permutation(N * N):
        r, d = k // N, k % N
        if r in send and rng.random() > zero: n[r, d] += min(rng.integers(0, CAPP + 1), CAPP - n[r, d], T - n[r].sum(), S - n[:, d].sum())
    return n
def stored(n):
    return np.stack([table(np.concatenate([n[r], np.zeros(16 - N, int)])) for r in range(N)])
def setup_inputs(rng):
    return {"x": f(rng, N, 128, 4 * T), "cn": stored(counts(rng)), "w": f(rng, N, 128, 512 * O)}
def setup_inputs_full(rng):
    n = np.zeros((N, N), int); a, b = rng.permutation(N), rng.permutation(N)
    for i in range(N):
        for j in range(min(T // CAPP, S // CAPP, N)): n[a[i], b[(i + j) % N]] = CAPP
    return {**setup_inputs(rng), "cn": stored(n)}
def setup_inputs_none(rng):
    n = counts(rng, zero=0.6, quiet=(int(rng.integers(0, N)),)); n[:, rng.integers(0, N)] = 0
    return {**setup_inputs(rng), "cn": stored(n)}
def setup_inputs_skew(rng):
    n = rng.integers(0, 4, (N, N)); n[rng.integers(0, N, N), np.arange(N)] = 4
    d = rng.integers(0, N); n[:, d] = 0; n[(d + rng.integers(1, N)) % N, d] = CAPP
    while n[:, d].sum() < S:
        q = rng.integers(0, N)
        if n[q, d] < CAPP: n[q, d] += 1
    return {**setup_inputs(rng), "cn": stored(n)}
def setup_inputs_last(rng):
    n = np.zeros((N, N), int)
    for r in (N - 2, N - 1):
        n[r] = 1
        while n[r].sum() < T:
            q = rng.integers(0, N)
            if n[r, q] < CAPP: n[r, q] += 1
    return {**setup_inputs(rng), "cn": stored(n)}
def setup_inputs_spread(rng):
    d = setup_inputs(rng); d["x"] = wide(rng, N, 128, 4 * T, cols=8); return d
def check_inputs(d):
    b = []
    e = np.stack([entries(d["cn"][r]) for r in range(N)]).astype(np.int64); n = e[:, :N]
    if n.min() < 0 or n.max() > CAPP: b.append("count")
    if (e[:, N:] != 0).any(): b.append("zeros")
    if (n.sum(axis=1) > T).any(): b.append("sent")
    if (n.sum(axis=0) > S).any(): b.append("received")
    return b
def reference(x, cn, w):
    n = np.stack([entries(cn[r])[:N] for r in range(N)])
    y = np.zeros((N, 128, O * S), np.float32); ln = np.zeros((N, 1, N + 1), np.float32)
    for d in range(N):
        ln[d, 0, 1:] = np.add.accumulate(n[:, d])
        k = int(np.add.reduce(n[:, d])); t = np.zeros((128, 4 * S), BF); at = 0
        for s in range(N):
            a, m = int(np.add.reduce(n[s, :d])), int(n[s, d])
            t[:, 4 * at:4 * (at + m)] = x[s][:, 4 * a:4 * (a + m)]; at += m
        q = mx_ref.quantize(t)
        for o in range(O): y[d][:, S * o:S * o + k] = mx_ref.matmul(mx_ref.quantize(np.ascontiguousarray(cut(w[d], o))), q)[:, :k]
    return {"y": y, "ln": ln}

@@ -1,0 +1,290 @@
+from concourse.bass import DstId, RemoteDMATransfer
+from concourse.mybir import dt, AluOpType, ActivationFunctionType
+
+N, T_COLS, CAPP, S_COLS, O = 8, 512, 128, 512, 4
+ZERO = N * CAPP
+PART = 320
+
+SCRATCH = {
+    "xt": ("sbuf", [128, 4 * T_COLS], "bfloat16"),
+    "wt": ("sbuf", [128, 512 * O], "bfloat16"),
+    "zt": ("sbuf", [128, 512], "bfloat16"),
+    "q": ("sbuf", [128, T_COLS], "float8_e4m3fn_x4"),
+    "qs": ("sbuf", [128, T_COLS], "uint8"),
+    "slot": ("sbuf", [128, N * CAPP], "float8_e4m3fn_x4"),
+    "slots": ("sbuf", [128, N * CAPP], "uint8"),
+    "land": ("sbuf", [128, ZERO + 128], "float8_e4m3fn_x4"),
+    "lands": ("sbuf", [128, ZERO + 128], "uint8"),
+    "wq": ("sbuf", [128, 128 * O], "float8_e4m3fn_x4"),
+    "wqs": ("sbuf", [128, 128 * O], "uint8"),
+    "pk": ("sbuf", [128, S_COLS], "float8_e4m3fn_x4"),
+    "pks": ("sbuf", [128, S_COLS], "uint8"),
+    "yo": ("sbuf", [128, O * S_COLS], "float32"),
+    "ps": ("psum", [128, 512 * 2 * O], "float32"),
+    "cn1": ("sbuf", [128, 16], "int32"),
+    "cnb": ("sbuf", [128, 16], "int32"),
+    "zi": ("sbuf", [128, 16], "int32"),
+    "pi": ("sbuf", [128, 8], "int32"),
+    "pm": ("sbuf", [128, 8], "int32"),
+    "p0": ("sbuf", [128, 8], "float32"),
+    "bi": ("sbuf", [128, 32], "int32"),
+    "base": ("sbuf", [128, 32], "float32"),
+    "inc": ("sbuf", [128, 64], "float32"),
+    "zf": ("sbuf", [128, 64], "float32"),
+    "sc": ("sbuf", [128, 64], "float32"),
+    "so": ("sbuf", [128, 64], "uint16"),
+    "cin": ("dram", [N, 128, 1], "int32"),
+    "cg": ("sbuf", [128, N * 128], "int32"),
+    "cf": ("sbuf", [128, 8], "float32"),
+    "lb": ("sbuf", [128, 24], "float32"),
+    "lbb": ("sbuf", [128, 24], "float32"),
+    "t8": ("sbuf", [128, 256], "float32"),
+    "ta": ("sbuf", [128, 128], "float32"),
+    "tb": ("sbuf", [128, 64], "float32"),
+    "tc": ("sbuf", [128, 32], "float32"),
+    "td": ("sbuf", [128, 32], "float32"),
+    "ro": ("sbuf", [128, 32], "uint16"),
+}
+SEMAPHORES = (["cn", "x0", "x1", "w", "ch", "cgot", "cg", "arrc", "arrs", "sent", "zi", "pi", "bi", "zt", "zq", "incm",
+               "zf", "lb0", "pm", "p0", "base", "bc", "i1", "sc", "so", "q0", "q1", "q2", "ownc", "owns", "wq", "cf",
+               "lb", "lbb", "t8", "ta", "tb", "tc", "td", "ro", "lnst", "yst"]
+              + ["pc%d" % i for i in range(6)] + ["pl%d" % i for i in range(6)]
+              + ["ac%d" % i for i in range(2)] + ["as%d" % i for i in range(2)]
+              + ["m%d" % i for i in range(2 * O)] + ["yv%d" % i for i in range(O)] + ["ys%d" % i for i in range(O)])
+
+
+def groups_of(r):
+    early = [[d] for d in range(2) if d != r]
+    rest = [d for d in range(2, N) if d != r]
+    if len(rest) == N - 2:
+        return early + [rest[0:2], rest[2:4], rest[4:6]]
+    return early + [rest[0:3], rest[3:5]]
+
+
+def count_engines(topo, cores, r):
+    dests = [d for d in range(N) if d != r]
+    e = topo.engines(cores[r], cores[dests[0]])
+    cut = {d: e[2 * k:2 * k + 2] for k, d in enumerate(dests)}
+    cut[dests[-1]] = e[2 * (len(dests) - 1):2 * (len(dests) - 1) + 4]
+    return cut
+
+
+def data_engines(topo, cores, r, group):
+    out = {}
+    for far in (True, False):
+        ds = [d for d in group if (topo.die(cores[d]) != topo.die(cores[r])) == far]
+        for k, d in enumerate(ds):
+            e = topo.engines(cores[r], cores[d])
+            a, b = (e[0::2], e[1::2]) if far else (e[1::2], e[0::2])
+            m = len(a)
+            while m * len(ds) > len(a):
+                m //= 2
+            out[d] = (a[m * k:m * k + m], b[m * k:m * k + m])
+    return out
+
+
+def bits(es):
+    return sum(1 << e for e in es)
+
+
+def runs(group):
+    out = []
+    for d in group:
+        if out and out[-1][1] == d:
+            out[-1][1] = d + 1
+        else:
+            out.append([d, d + 1])
+    return out
+
+
+def rank_program(g, core, T, topo):
+    r = T.rank_of(core)
+    if r is None:
+        return
+    cores = list(T.cores)
+    V, A, P, Y, sem = g.vector, g.scalar, g.tensor, g.sync, T.sem
+    copy = ActivationFunctionType.Copy
+    add, mx, mn, mul = AluOpType.add, AluOpType.max, AluOpType.min, AluOpType.mult
+    groups = groups_of(r)
+    sent = [0]
+
+    def send(items, rsem):
+        for it in items:
+            sent[0] += len(it[1])
+        if len(items) == 1:
+            d, es, src, dst = items[0]
+            rid, pid, _ = topo.addr(cores[d])
+            g.remote_dma(out_ap=dst, in_ap=src, remote_sem=rsem, local_sem=sem.sent, pid=pid, routing_id=rid,
+                         dma_engine_mask=bits(es))
+            return
+        tr = []
+        for d, es, src, dst in items:
+            rid, pid, _ = topo.addr(cores[d])
+            tr.append(RemoteDMATransfer(dst_ids=[DstId(rid=rid, pnc=pid)], dma_engine_mask=bits(es), remote_sem=rsem,
+                                        srcs=[src], dsts=[dst]))
+        g.remote_dma_fused(tr, local_sem=sem.sent)
+
+    h = 2 * T_COLS
+    Y.dma_start(T.cn1[0:1, 0:16], T.cn[:]).then_inc(sem.cn, 16)
+    Y.dma_start(T.xt[:, 0:h], T.x[:, 0:h]).then_inc(sem.x0, 16)
+    Y.dma_start(T.xt[:, h:2 * h], T.x[:, h:2 * h]).then_inc(sem.x1, 16)
+    Y.dma_start(T.wt[:], T.w[:]).then_inc(sem.w, 16)
+    A.dma_start(T.cin[r, 0:16, :], T.cn[:]).then_inc(sem.ch, 16)
+    V.memset(T.zi[:], 0).then_inc(sem.zi, 1)
+    A.wait_ge(sem.zi, 1)
+    A.dma_start(T.cin[r, 16:128, :], T.zi[0:7, 0:16]).then_inc(sem.ch, 16)
+
+    g.iota(T.pi[:, 0:1], [[1, 1]], 0, 1).then_inc(sem.pi, 1)
+    g.iota(T.bi[:], [[16, 32]], 0, 0).then_inc(sem.bi, 1)
+    V.memset(T.inc[:], 16.0).then_inc(sem.incm, 1)
+    V.memset(T.zf[:], 0.0).then_inc(sem.zf, 1)
+    V.memset(T.lb[0:1, 0:1], 0.0).then_inc(sem.lb0, 1)
+    V.memset(T.zt[:], 0.0).then_inc(sem.zt, 1)
+    V.wait_ge(sem.pi, 1)
+    V.tensor_scalar(T.pm[:, 0:1], T.pi[:, 0:1], 15, None, AluOpType.bitwise_and).then_inc(sem.pm, 1)
+    V.wait_ge(sem.pm, 1)
+    V.tensor_scalar(T.p0[:, 0:1], T.pm[:, 0:1], -16.0, None, add).then_inc(sem.p0, 1)
+    V.wait_ge(sem.p0, 1)
+    V.wait_ge(sem.bi, 1)
+    V.tensor_scalar(T.base[:], T.bi[:], T.p0[:, 0:1], 16.0, add, add).then_inc(sem.base, 1)
+    V.wait_ge(sem.zt, 1)
+    V.quantize_mx(T.land[:, ZERO:ZERO + 128], T.lands[:, ZERO:ZERO + 128], T.zt[:]).then_inc(sem.zq, 1)
+
+    g.wait_ge(sem.cn, 16)
+    g.partition_broadcast(T.cnb[:], T.cn1[0:1, 0:16], 128).then_inc(sem.bc, 1)
+    V.wait_ge(sem.bc, 1)
+    V.wait_ge(sem.incm, 1)
+    V.tensor_scalar(T.inc[:, 8:64:8], T.cnb[:, 0:7], -112.0, None, add).then_inc(sem.i1, 1)
+    V.wait_ge(sem.i1, 1)
+    V.wait_ge(sem.zf, 1)
+    V.tensor_tensor_scan(T.sc[:], T.inc[:], T.zf[:], T.p0[:, 0:1], add, mx).then_inc(sem.sc, 1)
+    V.wait_ge(sem.sc, 1)
+    V.tensor_scalar(T.so[:], T.sc[:], float(T_COLS - 1), None, mn).then_inc(sem.so, 1)
+
+    g.wait_ge(sem.ch, 32)
+    ce = count_engines(topo, cores, r)
+    send([(d, ce[d], T.cin[r], T.cin[r]) for d in ce], sem.cgot)
+
+    V.wait_ge(sem.x0, 16)
+    V.quantize_mx(T.q[:, 0:128], T.qs[:, 0:128], T.xt[:, 0:512]).then_inc(sem.q0, 1)
+    V.quantize_mx(T.q[:, 128:256], T.qs[:, 128:256], T.xt[:, 512:1024]).then_inc(sem.q1, 1)
+    V.wait_ge(sem.so, 1)
+    V.wait_ge(sem.q0, 1)
+    V.wait_ge(sem.q1, 1)
+    A.wait_ge(sem.so, 1)
+    A.wait_ge(sem.q0, 1)
+    A.wait_ge(sem.q1, 1)
+
+    def quantise_rest():
+        V.wait_ge(sem.x1, 16)
+        V.quantize_mx(T.q[:, 256:512], T.qs[:, 256:512], T.xt[:, 1024:2048]).then_inc(sem.q2, 1)
+        V.wait_ge(sem.q2, 1)
+        A.wait_ge(sem.q2, 1)
+
+    whole = False
+    for k, group in enumerate(groups):
+        if group[0] >= 2 and not whole:
+            quantise_rest()
+            whole = True
+        at = 0 if group == [0] else None
+        if at is None:
+            w = min(128 * (group[0] + 1), T_COLS) if len(group) == 1 else T_COLS
+            rr = runs(group)
+            for a, b in rr:
+                V.tensor_copy(T.slot[:, 128 * a:128 * b].bitcast(dt.uint32),
+                              T.q[:, 0:w].bitcast(dt.uint32).indirect(T.so[:, 8 * a:8 * b])).then_inc(sem["pc%d" % k], 1)
+                A.activation(T.slots[:, 128 * a:128 * b], T.qs[:, 0:w].indirect(T.so[:, 8 * a:8 * b]),
+                             copy).then_inc(sem["pl%d" % k], 1)
+        e = data_engines(topo, cores, r, group)
+        cs, ss = (T.q, T.qs) if at == 0 else (T.slot, T.slots)
+        if at == 0:
+            g.wait_ge(sem.q0, 1)
+        else:
+            g.wait_ge(sem["pc%d" % k], len(rr))
+        me = slice(128 * r, 128 * r + 128)
+        send([(d, e[d][0], cs[:, 128 * d:128 * d + 128].bitcast(dt.uint8), T.land[:, me].bitcast(dt.uint8))
+              for d in group], sem.arrc)
+        if at is None:
+            g.wait_ge(sem["pl%d" % k], len(rr))
+        send([(d, e[d][1], ss[:, 128 * d:128 * d + 128], T.lands[:, me]) for d in group], sem.arrs)
+
+    V.tensor_copy(T.land[:, 128 * r:128 * r + 128].bitcast(dt.uint32),
+                  T.q[:].bitcast(dt.uint32).indirect(T.so[:, 8 * r:8 * r + 8])).then_inc(sem.ownc, 1)
+    A.activation(T.lands[:, 128 * r:128 * r + 128], T.qs[:].indirect(T.so[:, 8 * r:8 * r + 8]), copy).then_inc(sem.owns, 1)
+    V.wait_ge(sem.w, 16)
+    V.quantize_mx(T.wq[:], T.wqs[:], T.wt[:]).then_inc(sem.wq, 1)
+
+    others = [s for s in range(N) if s != r]
+    Y.wait_ge(sem.ch, 32)
+    Y.wait_ge(sem.cgot, sum(len(count_engines(topo, cores, s)[r]) for s in others))
+    Y.dma_start(T.cg[0:1, :], T.cin[:]).then_inc(sem.cg, 16)
+    V.wait_ge(sem.cg, 16)
+    V.tensor_copy(T.cf[0:1, 0:8], T.cg[0:1, r:N * 128:128]).then_inc(sem.cf, 1)
+    V.wait_ge(sem.cf, 1)
+    V.tensor_tensor_scan(T.lb[0:1, 1:9], T.cf[0:1, 0:8], T.cf[0:1, 0:8], 0.0, add, mx).then_inc(sem.lb, 1)
+    V.tensor_scalar(T.lb[0:1, 9:17], T.cf[0:1, 0:8], -1.0, float(CAPP), mul, add).then_inc(sem.lb, 1)
+    g.wait_ge(sem.lb0, 1)
+    g.wait_ge(sem.lb, 2)
+    g.partition_broadcast(T.lbb[:, 0:17], T.lb[0:1, 0:17], 128).then_inc(sem.lbb, 1)
+    Y.wait_ge(sem.lb0, 1)
+    Y.wait_ge(sem.lb, 2)
+    Y.dma_start(T.ln[:], T.lb[0:1, 0:9]).then_inc(sem.lnst, 16)
+    V.wait_ge(sem.base, 1)
+    V.wait_ge(sem.lbb, 1)
+    for s in range(N):
+        V.tensor_scalar(T.t8[:, 32 * s:32 * s + 32], T.base[:], T.lbb[:, s + 1:s + 2], T.lbb[:, s + 9:s + 10],
+                        AluOpType.is_ge, mul).then_inc(sem.t8, 1)
+    V.wait_ge(sem.t8, N)
+    V.tensor_tensor(T.ta[:], T.t8[:, 0:128], T.t8[:, 128:256], add).then_inc(sem.ta, 1)
+    V.wait_ge(sem.ta, 1)
+    V.tensor_tensor(T.tb[:], T.ta[:, 0:64], T.ta[:, 64:128], add).then_inc(sem.tb, 1)
+    V.wait_ge(sem.tb, 1)
+    V.tensor_tensor(T.tc[:], T.tb[:, 0:32], T.tb[:, 32:64], add).then_inc(sem.tc, 1)
+    V.wait_ge(sem.tc, 1)
+    V.tensor_tensor(T.td[:], T.tc[:], T.base[:], add).then_inc(sem.td, 1)
+    V.wait_ge(sem.td, 1)
+    V.tensor_scalar(T.ro[:], T.td[:], float(ZERO), None, mn).then_inc(sem.ro, 1)
+
+    nc = ns = 0
+    for s in others:
+        for group in groups_of(s):
+            if r in group:
+                e = data_engines(topo, cores, s, group)[r]
+                nc, ns = nc + len(e[0]), ns + len(e[1])
+    for q in (V, A):
+        q.wait_ge(sem.ro, 1)
+        q.wait_ge(sem.zq, 1)
+    V.wait_ge(sem.ownc, 1)
+    A.wait_ge(sem.owns, 1)
+    V.wait_ge(sem.arrc, nc)
+    A.wait_ge(sem.arrs, ns)
+    parts = [(0, PART), (PART, S_COLS)]
+    for i, (a, b) in enumerate(parts):
+        V.tensor_copy(T.pk[:, a:b].bitcast(dt.uint32),
+                      T.land[:].bitcast(dt.uint32).indirect(T.ro[:, a // 16:b // 16])).then_inc(sem["ac%d" % i], 1)
+        A.activation(T.pks[:, a:b], T.lands[:].indirect(T.ro[:, a // 16:b // 16]), copy).then_inc(sem["as%d" % i], 1)
+
+    P.wait_ge(sem.wq, 1)
+    for o in range(O):
+        for i, (a, b) in enumerate(parts):
+            if o == 0:
+                P.wait_ge(sem["ac%d" % i], 1)
+                P.wait_ge(sem["as%d" % i], 1)
+            k = 2 * o + i
+            P.matmul_mx(T.ps[:, 512 * k:512 * k + b - a], T.wq[:, 128 * o:128 * o + 128],
+                        T.wqs[:, 128 * o:128 * o + 128], T.pk[:, a:b], T.pks[:, a:b], True,
+                        True).then_inc(sem["m%d" % k], 1)
+    for o in range(O):
+        at = S_COLS * o
+        V.wait_ge(sem["m%d" % (2 * o)], 1)
+        V.tensor_copy(T.yo[:, at:at + PART], T.ps[:, 1024 * o:1024 * o + PART]).then_inc(sem["yv%d" % o], 1)
+        A.wait_ge(sem["m%d" % (2 * o + 1)], 1)
+        A.activation(T.yo[:, at + PART:at + S_COLS], T.ps[:, 1024 * o + 512:1024 * o + 512 + S_COLS - PART],
+                     copy).then_inc(sem["ys%d" % o], 1)
+        Y.wait_ge(sem["yv%d" % o], 1)
+        Y.wait_ge(sem["ys%d" % o], 1)
+        Y.dma_start(T.y[:, at:at + S_COLS], T.yo[:, at:at + S_COLS]).then_inc(sem.yst, 16)
+
+    Y.wait_ge(sem.lnst, 16)
+    Y.wait_ge(sem.yst, 16 * O)
+    g.wait_ge(sem.sent, sent[0])

@@ -4,6 +4,7 @@ from concourse.mybir import dt, AluOpType, ActivationFunctionType
 N, T_COLS, CAPP, S_COLS, O = 8, 512, 128, 512, 4
 ZERO = N * CAPP
 PART = 320
+G = N + 1
 
 SCRATCH = {
     "xt": ("sbuf", [128, 4 * T_COLS], "bfloat16"),
@@ -34,20 +35,19 @@ SCRATCH = {
     "sc": ("sbuf", [128, 64], "float32"),
     "so": ("sbuf", [128, 64], "uint16"),
     "cin": ("dram", [N, 128, 1], "int32"),
-    "cg": ("sbuf", [128, N * 128], "int32"),
+    "cg": ("sbuf", [128, 16], "int32"),
+    "cgb": ("sbuf", [128, 16], "int32"),
     "cf": ("sbuf", [128, 8], "float32"),
-    "lb": ("sbuf", [128, 24], "float32"),
-    "lbb": ("sbuf", [128, 24], "float32"),
-    "t8": ("sbuf", [128, 256], "float32"),
-    "ta": ("sbuf", [128, 128], "float32"),
-    "tb": ("sbuf", [128, 64], "float32"),
-    "tc": ("sbuf", [128, 32], "float32"),
-    "td": ("sbuf", [128, 32], "float32"),
+    "mf": ("sbuf", [128, 8], "float32"),
+    "lb": ("sbuf", [128, 16], "float32"),
+    "keep": ("sbuf", [128, 32 * G], "float32"),
+    "t9": ("sbuf", [128, 32 * G], "float32"),
+    "s9": ("sbuf", [128, 32 * G], "float32"),
     "ro": ("sbuf", [128, 32], "uint16"),
 }
 SEMAPHORES = (["cn", "x0", "x1", "w", "ch", "cgot", "cg", "arrc", "arrs", "sent", "zi", "pi", "bi", "zt", "zq", "incm",
                "zf", "lb0", "pm", "p0", "base", "bc", "i1", "sc", "so", "q0", "q1", "q2", "ownc", "owns", "wq", "cf",
-               "lb", "lbb", "t8", "ta", "tb", "tc", "td", "ro", "lnst", "yst"]
+               "mf", "lb", "cgb", "k1", "k0", "t0", "t9", "s9", "ro", "lnst", "yst"]
               + ["pc%d" % i for i in range(6)] + ["pl%d" % i for i in range(6)]
               + ["ac%d" % i for i in range(2)] + ["as%d" % i for i in range(2)]
               + ["m%d" % i for i in range(2 * O)] + ["yv%d" % i for i in range(O)] + ["ys%d" % i for i in range(O)])
@@ -59,14 +59,6 @@ def groups_of(r):
     if len(rest) == N - 2:
         return early + [rest[0:2], rest[2:4], rest[4:6]]
     return early + [rest[0:3], rest[3:5]]
-
-
-def count_engines(topo, cores, r):
-    dests = [d for d in range(N) if d != r]
-    e = topo.engines(cores[r], cores[dests[0]])
-    cut = {d: e[2 * k:2 * k + 2] for k, d in enumerate(dests)}
-    cut[dests[-1]] = e[2 * (len(dests) - 1):2 * (len(dests) - 1) + 4]
-    return cut
 
 
 def data_engines(topo, cores, r, group):
@@ -102,11 +94,16 @@ def rank_program(g, core, T, topo):
     if r is None:
         return
     cores = list(T.cores)
+    others = [s for s in range(N) if s != r]
     V, A, P, Y, sem = g.vector, g.scalar, g.tensor, g.sync, T.sem
     copy = ActivationFunctionType.Copy
     add, mx, mn, mul = AluOpType.add, AluOpType.max, AluOpType.min, AluOpType.mult
     groups = groups_of(r)
     sent = [0]
+
+    def dst_id(d):
+        rid, pid, _ = topo.addr(cores[d])
+        return DstId(rid=rid, pnc=pid)
 
     def send(items, rsem):
         for it in items:
@@ -117,20 +114,17 @@ def rank_program(g, core, T, topo):
             g.remote_dma(out_ap=dst, in_ap=src, remote_sem=rsem, local_sem=sem.sent, pid=pid, routing_id=rid,
                          dma_engine_mask=bits(es))
             return
-        tr = []
-        for d, es, src, dst in items:
-            rid, pid, _ = topo.addr(cores[d])
-            tr.append(RemoteDMATransfer(dst_ids=[DstId(rid=rid, pnc=pid)], dma_engine_mask=bits(es), remote_sem=rsem,
-                                        srcs=[src], dsts=[dst]))
-        g.remote_dma_fused(tr, local_sem=sem.sent)
+        g.remote_dma_fused([RemoteDMATransfer(dst_ids=[dst_id(d)], dma_engine_mask=bits(es), remote_sem=rsem,
+                                              srcs=[src], dsts=[dst]) for d, es, src, dst in items],
+                           local_sem=sem.sent)
 
     h = 2 * T_COLS
     Y.dma_start(T.cn1[0:1, 0:16], T.cn[:]).then_inc(sem.cn, 16)
     Y.dma_start(T.xt[:, 0:h], T.x[:, 0:h]).then_inc(sem.x0, 16)
     Y.dma_start(T.xt[:, h:2 * h], T.x[:, h:2 * h]).then_inc(sem.x1, 16)
     Y.dma_start(T.wt[:], T.w[:]).then_inc(sem.w, 16)
-    A.dma_start(T.cin[r, 0:16, :], T.cn[:]).then_inc(sem.ch, 16)
     V.memset(T.zi[:], 0).then_inc(sem.zi, 1)
+    A.dma_start(T.cin[r, 0:16, :], T.cn[:]).then_inc(sem.ch, 16)
     A.wait_ge(sem.zi, 1)
     A.dma_start(T.cin[r, 16:128, :], T.zi[0:7, 0:16]).then_inc(sem.ch, 16)
 
@@ -138,8 +132,9 @@ def rank_program(g, core, T, topo):
     g.iota(T.bi[:], [[16, 32]], 0, 0).then_inc(sem.bi, 1)
     V.memset(T.inc[:], 16.0).then_inc(sem.incm, 1)
     V.memset(T.zf[:], 0.0).then_inc(sem.zf, 1)
-    V.memset(T.lb[0:1, 0:1], 0.0).then_inc(sem.lb0, 1)
+    V.memset(T.lb[:, 0:1], 0.0).then_inc(sem.lb0, 1)
     V.memset(T.zt[:], 0.0).then_inc(sem.zt, 1)
+    V.memset(T.keep[:], 1.0).then_inc(sem.k1, 1)
     V.wait_ge(sem.pi, 1)
     V.tensor_scalar(T.pm[:, 0:1], T.pi[:, 0:1], 15, None, AluOpType.bitwise_and).then_inc(sem.pm, 1)
     V.wait_ge(sem.pm, 1)
@@ -147,6 +142,9 @@ def rank_program(g, core, T, topo):
     V.wait_ge(sem.p0, 1)
     V.wait_ge(sem.bi, 1)
     V.tensor_scalar(T.base[:], T.bi[:], T.p0[:, 0:1], 16.0, add, add).then_inc(sem.base, 1)
+    V.tensor_scalar(T.t9[:, 0:32 * G:G], T.bi[:], T.p0[:, 0:1], 16.0, add, add).then_inc(sem.t0, 1)
+    V.wait_ge(sem.k1, 1)
+    V.memset(T.keep[:, 0:32 * G:G], 0.0).then_inc(sem.k0, 1)
     V.wait_ge(sem.zt, 1)
     V.quantize_mx(T.land[:, ZERO:ZERO + 128], T.lands[:, ZERO:ZERO + 128], T.zt[:]).then_inc(sem.zq, 1)
 
@@ -162,8 +160,11 @@ def rank_program(g, core, T, topo):
     V.tensor_scalar(T.so[:], T.sc[:], float(T_COLS - 1), None, mn).then_inc(sem.so, 1)
 
     g.wait_ge(sem.ch, 32)
-    ce = count_engines(topo, cores, r)
-    send([(d, ce[d], T.cin[r], T.cin[r]) for d in ce], sem.cgot)
+    g.remote_dma_fused([RemoteDMATransfer(dst_ids=[dst_id(d) for d in others],
+                                          dma_engine_mask=bits(topo.engines(core, cores[others[0]])[0:1]),
+                                          remote_sem=sem.cgot, srcs=[T.cin[r]], dsts=[T.cin[r] for d in others])],
+                       local_sem=sem.sent)
+    sent[0] += 1
 
     V.wait_ge(sem.x0, 16)
     V.quantize_mx(T.q[:, 0:128], T.qs[:, 0:128], T.xt[:, 0:512]).then_inc(sem.q0, 1)
@@ -182,68 +183,61 @@ def rank_program(g, core, T, topo):
         A.wait_ge(sem.q2, 1)
 
     whole = False
+    me = slice(128 * r, 128 * r + 128)
     for k, group in enumerate(groups):
         if group[0] >= 2 and not whole:
             quantise_rest()
             whole = True
-        at = 0 if group == [0] else None
-        if at is None:
-            w = min(128 * (group[0] + 1), T_COLS) if len(group) == 1 else T_COLS
-            rr = runs(group)
-            for a, b in rr:
-                V.tensor_copy(T.slot[:, 128 * a:128 * b].bitcast(dt.uint32),
-                              T.q[:, 0:w].bitcast(dt.uint32).indirect(T.so[:, 8 * a:8 * b])).then_inc(sem["pc%d" % k], 1)
-                A.activation(T.slots[:, 128 * a:128 * b], T.qs[:, 0:w].indirect(T.so[:, 8 * a:8 * b]),
-                             copy).then_inc(sem["pl%d" % k], 1)
+        rr = [] if group == [0] else runs(group)
+        w = min(128 * (group[0] + 1), T_COLS) if len(group) == 1 else T_COLS
+        for a, b in rr:
+            V.tensor_copy(T.slot[:, 128 * a:128 * b].bitcast(dt.uint32),
+                          T.q[:, 0:w].bitcast(dt.uint32).indirect(T.so[:, 8 * a:8 * b])).then_inc(sem["pc%d" % k], 1)
+            A.activation(T.slots[:, 128 * a:128 * b], T.qs[:, 0:w].indirect(T.so[:, 8 * a:8 * b]),
+                         copy).then_inc(sem["pl%d" % k], 1)
         e = data_engines(topo, cores, r, group)
-        cs, ss = (T.q, T.qs) if at == 0 else (T.slot, T.slots)
-        if at == 0:
-            g.wait_ge(sem.q0, 1)
-        else:
+        cs, ss = (T.slot, T.slots) if rr else (T.q, T.qs)
+        if rr:
             g.wait_ge(sem["pc%d" % k], len(rr))
-        me = slice(128 * r, 128 * r + 128)
+        else:
+            g.wait_ge(sem.q0, 1)
         send([(d, e[d][0], cs[:, 128 * d:128 * d + 128].bitcast(dt.uint8), T.land[:, me].bitcast(dt.uint8))
               for d in group], sem.arrc)
-        if at is None:
+        if rr:
             g.wait_ge(sem["pl%d" % k], len(rr))
         send([(d, e[d][1], ss[:, 128 * d:128 * d + 128], T.lands[:, me]) for d in group], sem.arrs)
 
-    V.tensor_copy(T.land[:, 128 * r:128 * r + 128].bitcast(dt.uint32),
+    V.tensor_copy(T.land[:, me].bitcast(dt.uint32),
                   T.q[:].bitcast(dt.uint32).indirect(T.so[:, 8 * r:8 * r + 8])).then_inc(sem.ownc, 1)
-    A.activation(T.lands[:, 128 * r:128 * r + 128], T.qs[:].indirect(T.so[:, 8 * r:8 * r + 8]), copy).then_inc(sem.owns, 1)
+    A.activation(T.lands[:, me], T.qs[:].indirect(T.so[:, 8 * r:8 * r + 8]), copy).then_inc(sem.owns, 1)
     V.wait_ge(sem.w, 16)
     V.quantize_mx(T.wq[:], T.wqs[:], T.wt[:]).then_inc(sem.wq, 1)
 
-    others = [s for s in range(N) if s != r]
     Y.wait_ge(sem.ch, 32)
-    Y.wait_ge(sem.cgot, sum(len(count_engines(topo, cores, s)[r]) for s in others))
-    Y.dma_start(T.cg[0:1, :], T.cin[:]).then_inc(sem.cg, 16)
-    V.wait_ge(sem.cg, 16)
-    V.tensor_copy(T.cf[0:1, 0:8], T.cg[0:1, r:N * 128:128]).then_inc(sem.cf, 1)
+    Y.wait_ge(sem.cgot, len(others))
+    Y.dma_start(T.cg[0:1, 0:16], T.cin[:, r:r + 2, 0]).then_inc(sem.cg, 16)
+    g.wait_ge(sem.cg, 16)
+    g.partition_broadcast(T.cgb[:], T.cg[0:1, 0:16], 128).then_inc(sem.cgb, 1)
+    V.wait_ge(sem.cgb, 1)
+    V.tensor_copy(T.cf[:], T.cgb[:, 0:16:2]).then_inc(sem.cf, 1)
+    V.tensor_scalar(T.mf[:], T.cgb[:, 0:16:2], -1.0, float(CAPP), mul, add).then_inc(sem.mf, 1)
     V.wait_ge(sem.cf, 1)
-    V.tensor_tensor_scan(T.lb[0:1, 1:9], T.cf[0:1, 0:8], T.cf[0:1, 0:8], 0.0, add, mx).then_inc(sem.lb, 1)
-    V.tensor_scalar(T.lb[0:1, 9:17], T.cf[0:1, 0:8], -1.0, float(CAPP), mul, add).then_inc(sem.lb, 1)
-    g.wait_ge(sem.lb0, 1)
-    g.wait_ge(sem.lb, 2)
-    g.partition_broadcast(T.lbb[:, 0:17], T.lb[0:1, 0:17], 128).then_inc(sem.lbb, 1)
-    Y.wait_ge(sem.lb0, 1)
-    Y.wait_ge(sem.lb, 2)
-    Y.dma_start(T.ln[:], T.lb[0:1, 0:9]).then_inc(sem.lnst, 16)
+    V.tensor_tensor_scan(T.lb[:, 1:9], T.cf[:], T.cf[:], 0.0, add, mx).then_inc(sem.lb, 1)
     V.wait_ge(sem.base, 1)
-    V.wait_ge(sem.lbb, 1)
+    V.wait_ge(sem.mf, 1)
+    V.wait_ge(sem.lb, 1)
     for s in range(N):
-        V.tensor_scalar(T.t8[:, 32 * s:32 * s + 32], T.base[:], T.lbb[:, s + 1:s + 2], T.lbb[:, s + 9:s + 10],
-                        AluOpType.is_ge, mul).then_inc(sem.t8, 1)
-    V.wait_ge(sem.t8, N)
-    V.tensor_tensor(T.ta[:], T.t8[:, 0:128], T.t8[:, 128:256], add).then_inc(sem.ta, 1)
-    V.wait_ge(sem.ta, 1)
-    V.tensor_tensor(T.tb[:], T.ta[:, 0:64], T.ta[:, 64:128], add).then_inc(sem.tb, 1)
-    V.wait_ge(sem.tb, 1)
-    V.tensor_tensor(T.tc[:], T.tb[:, 0:32], T.tb[:, 32:64], add).then_inc(sem.tc, 1)
-    V.wait_ge(sem.tc, 1)
-    V.tensor_tensor(T.td[:], T.tc[:], T.base[:], add).then_inc(sem.td, 1)
-    V.wait_ge(sem.td, 1)
-    V.tensor_scalar(T.ro[:], T.td[:], float(ZERO), None, mn).then_inc(sem.ro, 1)
+        V.tensor_scalar(T.t9[:, s + 1:32 * G:G], T.base[:], T.lb[:, s + 1:s + 2], T.mf[:, s:s + 1],
+                        AluOpType.is_ge, mul).then_inc(sem.t9, 1)
+    V.wait_ge(sem.k0, 1)
+    V.wait_ge(sem.t0, 1)
+    V.wait_ge(sem.t9, N)
+    V.tensor_tensor_scan(T.s9[:], T.keep[:], T.t9[:], 0.0, mul, add).then_inc(sem.s9, 1)
+    V.wait_ge(sem.s9, 1)
+    V.tensor_scalar(T.ro[:], T.s9[:, N:32 * G:G], float(ZERO), None, mn).then_inc(sem.ro, 1)
+    Y.wait_ge(sem.lb0, 1)
+    Y.wait_ge(sem.lb, 1)
+    Y.dma_start(T.ln[:], T.lb[0:1, 0:9]).then_inc(sem.lnst, 16)
 
     nc = ns = 0
     for s in others:

@@ -5,6 +5,7 @@ N, T_COLS, CAPP, S_COLS, O = 8, 512, 128, 512, 4
 ZERO = N * CAPP
 PART = 320
 G = N + 1
+SCALE_CALLS = [[0, 1], [2]]
 
 SCRATCH = {
     "xt": ("sbuf", [128, 4 * T_COLS], "bfloat16"),
@@ -45,34 +46,37 @@ SCRATCH = {
     "s9": ("sbuf", [128, 32 * G], "float32"),
     "ro": ("sbuf", [128, 32], "uint16"),
 }
-SEMAPHORES = (["cn", "x0", "x1", "w", "ch", "cgot", "cg", "arrc", "arrs", "sent", "zi", "pi", "bi", "zt", "zq", "incm",
-               "zf", "lb0", "pm", "p0", "base", "bc", "i1", "sc", "so", "q0", "q1", "q2", "ownc", "owns", "wq", "cf",
-               "mf", "lb", "cgb", "k1", "k0", "t0", "t9", "s9", "ro", "lnst", "yst"]
-              + ["pc%d" % i for i in range(6)] + ["pl%d" % i for i in range(6)]
+SEMAPHORES = (["cn", "x0", "x1", "w", "cgot", "arrc", "arrs", "sent", "pi", "bi", "zt", "zq", "incm", "cg", "cgb",
+               "ch", "zi", "zf", "lb0", "pm", "p0", "base", "bc", "i1", "sc", "so", "q0", "q1", "q2", "ownc", "owns",
+               "wq", "cf", "mf", "lb", "k1", "k0", "t0", "t9", "s9", "ro", "lnst", "yst"]
+              + ["pc%d" % i for i in range(3)] + ["pl%d" % i for i in range(3)]
               + ["ac%d" % i for i in range(2)] + ["as%d" % i for i in range(2)]
               + ["m%d" % i for i in range(2 * O)] + ["yv%d" % i for i in range(O)] + ["ys%d" % i for i in range(O)])
 
 
-def groups_of(r):
-    early = [[d] for d in range(2) if d != r]
+def groups_of(topo, cores, r):
+    first = [d for d in range(2) if d != r]
     rest = [d for d in range(2, N) if d != r]
-    if len(rest) == N - 2:
-        return early + [rest[0:2], rest[2:4], rest[4:6]]
-    return early + [rest[0:3], rest[3:5]]
+    near = [d for d in rest if topo.die(cores[d]) == topo.die(cores[r])]
+    far = [d for d in rest if d not in near]
+    return [first, [near[0], far[0]], near[1:] + far[1:]]
 
 
-def data_engines(topo, cores, r, group):
-    out = {}
-    for far in (True, False):
-        ds = [d for d in group if (topo.die(cores[d]) != topo.die(cores[r])) == far]
-        for k, d in enumerate(ds):
-            e = topo.engines(cores[r], cores[d])
-            a, b = (e[0::2], e[1::2]) if far else (e[1::2], e[0::2])
-            m = len(a)
-            while m * len(ds) > len(a):
-                m //= 2
-            out[d] = (a[m * k:m * k + m], b[m * k:m * k + m])
-    return out
+def engines_for(topo, cores, r, group, scales):
+    e = topo.engines(cores[r], cores[group[0]])
+    if len(group) == 1:
+        return {group[0]: e}
+    fars = [d for d in group if topo.die(cores[d]) != topo.die(cores[r])]
+    nears = [d for d in group if d not in fars]
+    a, b = (e[1::2], e[0::2]) if scales else (e[0::2], e[1::2])
+    h = len(a) // 2
+    if len(group) == 2:
+        cut = [a, b]
+    elif len(group) == 3:
+        cut = [b[:h], b[h:], a] if len(fars) == 2 else [a, b[:h], b[h:]]
+    else:
+        cut = [a[:h], a[h:], b[:h], b[h:]]
+    return {d: c for d, c in zip(fars + nears, cut)}
 
 
 def bits(es):
@@ -81,7 +85,7 @@ def bits(es):
 
 def runs(group):
     out = []
-    for d in group:
+    for d in sorted(group):
         if out and out[-1][1] == d:
             out[-1][1] = d + 1
         else:
@@ -98,7 +102,7 @@ def rank_program(g, core, T, topo):
     V, A, P, Y, sem = g.vector, g.scalar, g.tensor, g.sync, T.sem
     copy = ActivationFunctionType.Copy
     add, mx, mn, mul = AluOpType.add, AluOpType.max, AluOpType.min, AluOpType.mult
-    groups = groups_of(r)
+    groups = groups_of(topo, cores, r)
     sent = [0]
 
     def dst_id(d):
@@ -120,33 +124,26 @@ def rank_program(g, core, T, topo):
 
     h = 2 * T_COLS
     Y.dma_start(T.cn1[0:1, 0:16], T.cn[:]).then_inc(sem.cn, 16)
+    A.dma_start(T.cin[r, 0:16, :], T.cn[:]).then_inc(sem.ch, 16)
+    V.memset(T.zi[:], 0).then_inc(sem.zi, 1)
+    A.wait_ge(sem.zi, 1)
+    A.dma_start(T.cin[r, 16:128, :], T.zi[0:7, 0:16]).then_inc(sem.ch, 16)
+    Y.wait_ge(sem.zi, 1)
     Y.dma_start(T.xt[:, 0:h], T.x[:, 0:h]).then_inc(sem.x0, 16)
     Y.dma_start(T.xt[:, h:2 * h], T.x[:, h:2 * h]).then_inc(sem.x1, 16)
     Y.dma_start(T.wt[:], T.w[:]).then_inc(sem.w, 16)
-    V.memset(T.zi[:], 0).then_inc(sem.zi, 1)
-    A.dma_start(T.cin[r, 0:16, :], T.cn[:]).then_inc(sem.ch, 16)
-    A.wait_ge(sem.zi, 1)
-    A.dma_start(T.cin[r, 16:128, :], T.zi[0:7, 0:16]).then_inc(sem.ch, 16)
 
     g.iota(T.pi[:, 0:1], [[1, 1]], 0, 1).then_inc(sem.pi, 1)
     g.iota(T.bi[:], [[16, 32]], 0, 0).then_inc(sem.bi, 1)
     V.memset(T.inc[:], 16.0).then_inc(sem.incm, 1)
     V.memset(T.zf[:], 0.0).then_inc(sem.zf, 1)
-    V.memset(T.lb[:, 0:1], 0.0).then_inc(sem.lb0, 1)
-    V.memset(T.zt[:], 0.0).then_inc(sem.zt, 1)
-    V.memset(T.keep[:], 1.0).then_inc(sem.k1, 1)
     V.wait_ge(sem.pi, 1)
     V.tensor_scalar(T.pm[:, 0:1], T.pi[:, 0:1], 15, None, AluOpType.bitwise_and).then_inc(sem.pm, 1)
     V.wait_ge(sem.pm, 1)
     V.tensor_scalar(T.p0[:, 0:1], T.pm[:, 0:1], -16.0, None, add).then_inc(sem.p0, 1)
-    V.wait_ge(sem.p0, 1)
-    V.wait_ge(sem.bi, 1)
-    V.tensor_scalar(T.base[:], T.bi[:], T.p0[:, 0:1], 16.0, add, add).then_inc(sem.base, 1)
-    V.tensor_scalar(T.t9[:, 0:32 * G:G], T.bi[:], T.p0[:, 0:1], 16.0, add, add).then_inc(sem.t0, 1)
-    V.wait_ge(sem.k1, 1)
-    V.memset(T.keep[:, 0:32 * G:G], 0.0).then_inc(sem.k0, 1)
-    V.wait_ge(sem.zt, 1)
-    V.quantize_mx(T.land[:, ZERO:ZERO + 128], T.lands[:, ZERO:ZERO + 128], T.zt[:]).then_inc(sem.zq, 1)
+    V.memset(T.lb[:, 0:1], 0.0).then_inc(sem.lb0, 1)
+    V.memset(T.keep[:], 1.0).then_inc(sem.k1, 1)
+    V.memset(T.zt[:], 0.0).then_inc(sem.zt, 1)
 
     g.wait_ge(sem.cn, 16)
     g.partition_broadcast(T.cnb[:], T.cn1[0:1, 0:16], 128).then_inc(sem.bc, 1)
@@ -155,6 +152,7 @@ def rank_program(g, core, T, topo):
     V.tensor_scalar(T.inc[:, 8:64:8], T.cnb[:, 0:7], -112.0, None, add).then_inc(sem.i1, 1)
     V.wait_ge(sem.i1, 1)
     V.wait_ge(sem.zf, 1)
+    V.wait_ge(sem.p0, 1)
     V.tensor_tensor_scan(T.sc[:], T.inc[:], T.zf[:], T.p0[:, 0:1], add, mx).then_inc(sem.sc, 1)
     V.wait_ge(sem.sc, 1)
     V.tensor_scalar(T.so[:], T.sc[:], float(T_COLS - 1), None, mn).then_inc(sem.so, 1)
@@ -165,6 +163,9 @@ def rank_program(g, core, T, topo):
                                           remote_sem=sem.cgot, srcs=[T.cin[r]], dsts=[T.cin[r] for d in others])],
                        local_sem=sem.sent)
     sent[0] += 1
+    Y.wait_ge(sem.ch, 32)
+    Y.wait_ge(sem.cgot, len(others))
+    Y.dma_start(T.cg[0:1, 0:16], T.cin[:, r:r + 2, 0]).then_inc(sem.cg, 16)
 
     V.wait_ge(sem.x0, 16)
     V.quantize_mx(T.q[:, 0:128], T.qs[:, 0:128], T.xt[:, 0:512]).then_inc(sem.q0, 1)
@@ -176,48 +177,55 @@ def rank_program(g, core, T, topo):
     A.wait_ge(sem.q0, 1)
     A.wait_ge(sem.q1, 1)
 
-    def quantise_rest():
-        V.wait_ge(sem.x1, 16)
-        V.quantize_mx(T.q[:, 256:512], T.qs[:, 256:512], T.xt[:, 1024:2048]).then_inc(sem.q2, 1)
-        V.wait_ge(sem.q2, 1)
-        A.wait_ge(sem.q2, 1)
-
-    whole = False
     me = slice(128 * r, 128 * r + 128)
+    picks = []
     for k, group in enumerate(groups):
-        if group[0] >= 2 and not whole:
-            quantise_rest()
-            whole = True
-        rr = [] if group == [0] else runs(group)
-        w = min(128 * (group[0] + 1), T_COLS) if len(group) == 1 else T_COLS
+        if k == 1:
+            V.wait_ge(sem.bi, 1)
+            V.tensor_scalar(T.base[:], T.bi[:], T.p0[:, 0:1], 16.0, add, add).then_inc(sem.base, 1)
+            V.tensor_scalar(T.t9[:, 0:32 * G:G], T.bi[:], T.p0[:, 0:1], 16.0, add, add).then_inc(sem.t0, 1)
+            V.wait_ge(sem.x1, 16)
+            V.quantize_mx(T.q[:, 256:512], T.qs[:, 256:512], T.xt[:, 1024:2048]).then_inc(sem.q2, 1)
+            V.wait_ge(sem.q2, 1)
+            A.wait_ge(sem.q2, 1)
+        w = 256 if k == 0 else T_COLS
+        rr = runs([d for d in group if d != 0])
+        picks.append(len(rr))
         for a, b in rr:
             V.tensor_copy(T.slot[:, 128 * a:128 * b].bitcast(dt.uint32),
                           T.q[:, 0:w].bitcast(dt.uint32).indirect(T.so[:, 8 * a:8 * b])).then_inc(sem["pc%d" % k], 1)
             A.activation(T.slots[:, 128 * a:128 * b], T.qs[:, 0:w].indirect(T.so[:, 8 * a:8 * b]),
                          copy).then_inc(sem["pl%d" % k], 1)
-        e = data_engines(topo, cores, r, group)
-        cs, ss = (T.slot, T.slots) if rr else (T.q, T.qs)
+        if 0 in group:
+            g.wait_ge(sem.q0, 1)
         if rr:
             g.wait_ge(sem["pc%d" % k], len(rr))
-        else:
-            g.wait_ge(sem.q0, 1)
-        send([(d, e[d][0], cs[:, 128 * d:128 * d + 128].bitcast(dt.uint8), T.land[:, me].bitcast(dt.uint8))
-              for d in group], sem.arrc)
-        if rr:
-            g.wait_ge(sem["pl%d" % k], len(rr))
-        send([(d, e[d][1], ss[:, 128 * d:128 * d + 128], T.lands[:, me]) for d in group], sem.arrs)
+        e = engines_for(topo, cores, r, group, False)
+        send([(d, e[d], (T.slot if d else T.q)[:, 128 * d:128 * d + 128].bitcast(dt.uint8),
+               T.land[:, me].bitcast(dt.uint8)) for d in group], sem.arrc)
+        if k == len(groups) - 1:
+            g.wait_ge(sem.cg, 16)
+            g.partition_broadcast(T.cgb[:], T.cg[0:1, 0:16], 128).then_inc(sem.cgb, 1)
+        for ks in SCALE_CALLS:
+            if ks[-1] == k:
+                for j in ks:
+                    if picks[j]:
+                        g.wait_ge(sem["pl%d" % j], picks[j])
+                both = [d for j in ks for d in groups[j]]
+                e = engines_for(topo, cores, r, both, True)
+                send([(d, e[d], (T.slots if d else T.qs)[:, 128 * d:128 * d + 128], T.lands[:, me]) for d in both],
+                     sem.arrs)
 
     V.tensor_copy(T.land[:, me].bitcast(dt.uint32),
                   T.q[:].bitcast(dt.uint32).indirect(T.so[:, 8 * r:8 * r + 8])).then_inc(sem.ownc, 1)
     A.activation(T.lands[:, me], T.qs[:].indirect(T.so[:, 8 * r:8 * r + 8]), copy).then_inc(sem.owns, 1)
+    V.wait_ge(sem.k1, 1)
+    V.memset(T.keep[:, 0:32 * G:G], 0.0).then_inc(sem.k0, 1)
+    V.wait_ge(sem.zt, 1)
+    V.quantize_mx(T.land[:, ZERO:ZERO + 128], T.lands[:, ZERO:ZERO + 128], T.zt[:]).then_inc(sem.zq, 1)
     V.wait_ge(sem.w, 16)
     V.quantize_mx(T.wq[:], T.wqs[:], T.wt[:]).then_inc(sem.wq, 1)
 
-    Y.wait_ge(sem.ch, 32)
-    Y.wait_ge(sem.cgot, len(others))
-    Y.dma_start(T.cg[0:1, 0:16], T.cin[:, r:r + 2, 0]).then_inc(sem.cg, 16)
-    g.wait_ge(sem.cg, 16)
-    g.partition_broadcast(T.cgb[:], T.cg[0:1, 0:16], 128).then_inc(sem.cgb, 1)
     V.wait_ge(sem.cgb, 1)
     V.tensor_copy(T.cf[:], T.cgb[:, 0:16:2]).then_inc(sem.cf, 1)
     V.tensor_scalar(T.mf[:], T.cgb[:, 0:16:2], -1.0, float(CAPP), mul, add).then_inc(sem.mf, 1)
@@ -241,10 +249,14 @@ def rank_program(g, core, T, topo):
 
     nc = ns = 0
     for s in others:
-        for group in groups_of(s):
+        gs = groups_of(topo, cores, s)
+        for group in gs:
             if r in group:
-                e = data_engines(topo, cores, s, group)[r]
-                nc, ns = nc + len(e[0]), ns + len(e[1])
+                nc += len(engines_for(topo, cores, s, group, False)[r])
+        for ks in SCALE_CALLS:
+            both = [d for j in ks for d in gs[j]]
+            if r in both:
+                ns += len(engines_for(topo, cores, s, both, True)[r])
     for q in (V, A):
         q.wait_ge(sem.ro, 1)
         q.wait_ge(sem.zq, 1)
@@ -268,6 +280,7 @@ def rank_program(g, core, T, topo):
             P.matmul_mx(T.ps[:, 512 * k:512 * k + b - a], T.wq[:, 128 * o:128 * o + 128],
                         T.wqs[:, 128 * o:128 * o + 128], T.pk[:, a:b], T.pks[:, a:b], True,
                         True).then_inc(sem["m%d" % k], 1)
+    stores = 0
     for o in range(O):
         at = S_COLS * o
         V.wait_ge(sem["m%d" % (2 * o)], 1)
@@ -275,10 +288,14 @@ def rank_program(g, core, T, topo):
         A.wait_ge(sem["m%d" % (2 * o + 1)], 1)
         A.activation(T.yo[:, at + PART:at + S_COLS], T.ps[:, 1024 * o + 512:1024 * o + 512 + S_COLS - PART],
                      copy).then_inc(sem["ys%d" % o], 1)
+        cuts = [0, PART, S_COLS] if o == 0 else [0, S_COLS]
         Y.wait_ge(sem["yv%d" % o], 1)
-        Y.wait_ge(sem["ys%d" % o], 1)
-        Y.dma_start(T.y[:, at:at + S_COLS], T.yo[:, at:at + S_COLS]).then_inc(sem.yst, 16)
+        for a, b in zip(cuts, cuts[1:]):
+            if b == S_COLS:
+                Y.wait_ge(sem["ys%d" % o], 1)
+            Y.dma_start(T.y[:, at + a:at + b], T.yo[:, at + a:at + b]).then_inc(sem.yst, 16)
+            stores += 1
 
     Y.wait_ge(sem.lnst, 16)
-    Y.wait_ge(sem.yst, 16 * O)
+    Y.wait_ge(sem.yst, 16 * stores)
     g.wait_ge(sem.sent, sent[0])

from concourse.bass import DstId, RemoteDMATransfer
from concourse.mybir import dt, AluOpType, ActivationFunctionType

N, T_COLS, CAPP, S_COLS, O = 8, 512, 128, 512, 4
ZERO = N * CAPP
PART = 320
G = N + 1
SCALE_CALLS = [[0, 1], [2]]

SCRATCH = {
    "xt": ("sbuf", [128, 4 * T_COLS], "bfloat16"),
    "wt": ("sbuf", [128, 512 * O], "bfloat16"),
    "zt": ("sbuf", [128, 512], "bfloat16"),
    "q": ("sbuf", [128, T_COLS], "float8_e4m3fn_x4"),
    "qs": ("sbuf", [128, T_COLS], "uint8"),
    "slot": ("sbuf", [128, N * CAPP], "float8_e4m3fn_x4"),
    "slots": ("sbuf", [128, N * CAPP], "uint8"),
    "land": ("sbuf", [128, ZERO + 128], "float8_e4m3fn_x4"),
    "lands": ("sbuf", [128, ZERO + 128], "uint8"),
    "wq": ("sbuf", [128, 128 * O], "float8_e4m3fn_x4"),
    "wqs": ("sbuf", [128, 128 * O], "uint8"),
    "pk": ("sbuf", [128, S_COLS], "float8_e4m3fn_x4"),
    "pks": ("sbuf", [128, S_COLS], "uint8"),
    "yo": ("sbuf", [128, O * S_COLS], "float32"),
    "ps": ("psum", [128, 512 * 2 * O], "float32"),
    "cn1": ("sbuf", [128, 16], "int32"),
    "cnb": ("sbuf", [128, 16], "int32"),
    "zi": ("sbuf", [128, 16], "int32"),
    "pi": ("sbuf", [128, 8], "int32"),
    "pm": ("sbuf", [128, 8], "int32"),
    "p0": ("sbuf", [128, 8], "float32"),
    "bi": ("sbuf", [128, 32], "int32"),
    "base": ("sbuf", [128, 32], "float32"),
    "inc": ("sbuf", [128, 64], "float32"),
    "zf": ("sbuf", [128, 64], "float32"),
    "sc": ("sbuf", [128, 64], "float32"),
    "so": ("sbuf", [128, 64], "uint16"),
    "cin": ("dram", [N, 128, 1], "int32"),
    "cg": ("sbuf", [128, 16], "int32"),
    "cgb": ("sbuf", [128, 16], "int32"),
    "cf": ("sbuf", [128, 8], "float32"),
    "mf": ("sbuf", [128, 8], "float32"),
    "lb": ("sbuf", [128, 16], "float32"),
    "keep": ("sbuf", [128, 32 * G], "float32"),
    "t9": ("sbuf", [128, 32 * G], "float32"),
    "s9": ("sbuf", [128, 32 * G], "float32"),
    "ro": ("sbuf", [128, 32], "uint16"),
}
SEMAPHORES = (["cn", "x0", "x1", "w", "cgot", "arrc", "arrs", "sent", "pi", "bi", "zt", "zq", "incm", "cg", "cgb",
               "ch", "zi", "zf", "lb0", "pm", "p0", "base", "bc", "i1", "sc", "so", "q0", "q1", "q2", "ownc", "owns",
               "wq", "cf", "mf", "lb", "k1", "k0", "t0", "t9", "s9", "ro", "lnst", "yst"]
              + ["pc%d" % i for i in range(3)] + ["pl%d" % i for i in range(3)]
              + ["ac%d" % i for i in range(2)] + ["as%d" % i for i in range(2)]
              + ["m%d" % i for i in range(2 * O)] + ["yv%d" % i for i in range(O)] + ["ys%d" % i for i in range(O)])


def groups_of(topo, cores, r):
    first = [d for d in range(2) if d != r]
    rest = [d for d in range(2, N) if d != r]
    near = [d for d in rest if topo.die(cores[d]) == topo.die(cores[r])]
    far = [d for d in rest if d not in near]
    return [first, [near[0], far[0]], near[1:] + far[1:]]


def engines_for(topo, cores, r, group, scales):
    e = topo.engines(cores[r], cores[group[0]])
    if len(group) == 1:
        return {group[0]: e}
    fars = [d for d in group if topo.die(cores[d]) != topo.die(cores[r])]
    nears = [d for d in group if d not in fars]
    a, b = (e[1::2], e[0::2]) if scales else (e[0::2], e[1::2])
    h = len(a) // 2
    if len(group) == 2:
        cut = [a, b]
    elif len(group) == 3:
        cut = [b[:h], b[h:], a] if len(fars) == 2 else [a, b[:h], b[h:]]
    else:
        cut = [a[:h], a[h:], b[:h], b[h:]]
    return {d: c for d, c in zip(fars + nears, cut)}


def bits(es):
    return sum(1 << e for e in es)


def runs(group):
    out = []
    for d in sorted(group):
        if out and out[-1][1] == d:
            out[-1][1] = d + 1
        else:
            out.append([d, d + 1])
    return out


def rank_program(g, core, T, topo):
    r = T.rank_of(core)
    if r is None:
        return
    cores = list(T.cores)
    others = [s for s in range(N) if s != r]
    V, A, P, Y, sem = g.vector, g.scalar, g.tensor, g.sync, T.sem
    copy = ActivationFunctionType.Copy
    add, mx, mn, mul = AluOpType.add, AluOpType.max, AluOpType.min, AluOpType.mult
    groups = groups_of(topo, cores, r)
    sent = [0]

    def dst_id(d):
        rid, pid, _ = topo.addr(cores[d])
        return DstId(rid=rid, pnc=pid)

    def send(items, rsem):
        for it in items:
            sent[0] += len(it[1])
        if len(items) == 1:
            d, es, src, dst = items[0]
            rid, pid, _ = topo.addr(cores[d])
            g.remote_dma(out_ap=dst, in_ap=src, remote_sem=rsem, local_sem=sem.sent, pid=pid, routing_id=rid,
                         dma_engine_mask=bits(es))
            return
        g.remote_dma_fused([RemoteDMATransfer(dst_ids=[dst_id(d)], dma_engine_mask=bits(es), remote_sem=rsem,
                                              srcs=[src], dsts=[dst]) for d, es, src, dst in items],
                           local_sem=sem.sent)

    h = 2 * T_COLS
    Y.dma_start(T.cn1[0:1, 0:16], T.cn[:]).then_inc(sem.cn, 16)
    A.dma_start(T.cin[r, 0:16, :], T.cn[:]).then_inc(sem.ch, 16)
    V.memset(T.zi[:], 0).then_inc(sem.zi, 1)
    A.wait_ge(sem.zi, 1)
    A.dma_start(T.cin[r, 16:128, :], T.zi[0:7, 0:16]).then_inc(sem.ch, 16)
    Y.wait_ge(sem.zi, 1)
    Y.dma_start(T.xt[:, 0:h], T.x[:, 0:h]).then_inc(sem.x0, 16)
    Y.dma_start(T.xt[:, h:2 * h], T.x[:, h:2 * h]).then_inc(sem.x1, 16)
    Y.dma_start(T.wt[:], T.w[:]).then_inc(sem.w, 16)

    g.iota(T.pi[:, 0:1], [[1, 1]], 0, 1).then_inc(sem.pi, 1)
    g.iota(T.bi[:], [[16, 32]], 0, 0).then_inc(sem.bi, 1)
    V.memset(T.inc[:], 16.0).then_inc(sem.incm, 1)
    V.memset(T.zf[:], 0.0).then_inc(sem.zf, 1)
    V.wait_ge(sem.pi, 1)
    V.tensor_scalar(T.pm[:, 0:1], T.pi[:, 0:1], 15, None, AluOpType.bitwise_and).then_inc(sem.pm, 1)
    V.wait_ge(sem.pm, 1)
    V.tensor_scalar(T.p0[:, 0:1], T.pm[:, 0:1], -16.0, None, add).then_inc(sem.p0, 1)
    V.memset(T.lb[:, 0:1], 0.0).then_inc(sem.lb0, 1)
    V.memset(T.keep[:], 1.0).then_inc(sem.k1, 1)
    V.memset(T.zt[:], 0.0).then_inc(sem.zt, 1)

    g.wait_ge(sem.cn, 16)
    g.partition_broadcast(T.cnb[:], T.cn1[0:1, 0:16], 128).then_inc(sem.bc, 1)
    V.wait_ge(sem.bc, 1)
    V.wait_ge(sem.incm, 1)
    V.tensor_scalar(T.inc[:, 8:64:8], T.cnb[:, 0:7], -112.0, None, add).then_inc(sem.i1, 1)
    V.wait_ge(sem.i1, 1)
    V.wait_ge(sem.zf, 1)
    V.wait_ge(sem.p0, 1)
    V.tensor_tensor_scan(T.sc[:], T.inc[:], T.zf[:], T.p0[:, 0:1], add, mx).then_inc(sem.sc, 1)
    V.wait_ge(sem.sc, 1)
    V.tensor_scalar(T.so[:], T.sc[:], float(T_COLS - 1), None, mn).then_inc(sem.so, 1)

    g.wait_ge(sem.ch, 32)
    g.remote_dma_fused([RemoteDMATransfer(dst_ids=[dst_id(d) for d in others],
                                          dma_engine_mask=bits(topo.engines(core, cores[others[0]])[0:1]),
                                          remote_sem=sem.cgot, srcs=[T.cin[r]], dsts=[T.cin[r] for d in others])],
                       local_sem=sem.sent)
    sent[0] += 1
    Y.wait_ge(sem.ch, 32)
    Y.wait_ge(sem.cgot, len(others))
    Y.dma_start(T.cg[0:1, 0:16], T.cin[:, r:r + 2, 0]).then_inc(sem.cg, 16)

    V.wait_ge(sem.x0, 16)
    V.quantize_mx(T.q[:, 0:128], T.qs[:, 0:128], T.xt[:, 0:512]).then_inc(sem.q0, 1)
    V.quantize_mx(T.q[:, 128:256], T.qs[:, 128:256], T.xt[:, 512:1024]).then_inc(sem.q1, 1)
    V.wait_ge(sem.so, 1)
    V.wait_ge(sem.q0, 1)
    V.wait_ge(sem.q1, 1)
    A.wait_ge(sem.so, 1)
    A.wait_ge(sem.q0, 1)
    A.wait_ge(sem.q1, 1)

    me = slice(128 * r, 128 * r + 128)
    picks = []
    for k, group in enumerate(groups):
        if k == 1:
            V.wait_ge(sem.bi, 1)
            V.tensor_scalar(T.base[:], T.bi[:], T.p0[:, 0:1], 16.0, add, add).then_inc(sem.base, 1)
            V.tensor_scalar(T.t9[:, 0:32 * G:G], T.bi[:], T.p0[:, 0:1], 16.0, add, add).then_inc(sem.t0, 1)
            V.wait_ge(sem.x1, 16)
            V.quantize_mx(T.q[:, 256:512], T.qs[:, 256:512], T.xt[:, 1024:2048]).then_inc(sem.q2, 1)
            V.wait_ge(sem.q2, 1)
            A.wait_ge(sem.q2, 1)
        w = 256 if k == 0 else T_COLS
        rr = runs([d for d in group if d != 0])
        picks.append(len(rr))
        for a, b in rr:
            V.tensor_copy(T.slot[:, 128 * a:128 * b].bitcast(dt.uint32),
                          T.q[:, 0:w].bitcast(dt.uint32).indirect(T.so[:, 8 * a:8 * b])).then_inc(sem["pc%d" % k], 1)
            A.activation(T.slots[:, 128 * a:128 * b], T.qs[:, 0:w].indirect(T.so[:, 8 * a:8 * b]),
                         copy).then_inc(sem["pl%d" % k], 1)
        if 0 in group:
            g.wait_ge(sem.q0, 1)
        if rr:
            g.wait_ge(sem["pc%d" % k], len(rr))
        e = engines_for(topo, cores, r, group, False)
        send([(d, e[d], (T.slot if d else T.q)[:, 128 * d:128 * d + 128].bitcast(dt.uint8),
               T.land[:, me].bitcast(dt.uint8)) for d in group], sem.arrc)
        if k == len(groups) - 1:
            g.wait_ge(sem.cg, 16)
            g.partition_broadcast(T.cgb[:], T.cg[0:1, 0:16], 128).then_inc(sem.cgb, 1)
        for ks in SCALE_CALLS:
            if ks[-1] == k:
                for j in ks:
                    if picks[j]:
                        g.wait_ge(sem["pl%d" % j], picks[j])
                both = [d for j in ks for d in groups[j]]
                e = engines_for(topo, cores, r, both, True)
                send([(d, e[d], (T.slots if d else T.qs)[:, 128 * d:128 * d + 128], T.lands[:, me]) for d in both],
                     sem.arrs)

    V.tensor_copy(T.land[:, me].bitcast(dt.uint32),
                  T.q[:].bitcast(dt.uint32).indirect(T.so[:, 8 * r:8 * r + 8])).then_inc(sem.ownc, 1)
    A.activation(T.lands[:, me], T.qs[:].indirect(T.so[:, 8 * r:8 * r + 8]), copy).then_inc(sem.owns, 1)
    V.wait_ge(sem.k1, 1)
    V.memset(T.keep[:, 0:32 * G:G], 0.0).then_inc(sem.k0, 1)
    V.wait_ge(sem.zt, 1)
    V.quantize_mx(T.land[:, ZERO:ZERO + 128], T.lands[:, ZERO:ZERO + 128], T.zt[:]).then_inc(sem.zq, 1)
    V.wait_ge(sem.w, 16)
    V.quantize_mx(T.wq[:], T.wqs[:], T.wt[:]).then_inc(sem.wq, 1)

    V.wait_ge(sem.cgb, 1)
    V.tensor_copy(T.cf[:], T.cgb[:, 0:16:2]).then_inc(sem.cf, 1)
    V.tensor_scalar(T.mf[:], T.cgb[:, 0:16:2], -1.0, float(CAPP), mul, add).then_inc(sem.mf, 1)
    V.wait_ge(sem.cf, 1)
    V.tensor_tensor_scan(T.lb[:, 1:9], T.cf[:], T.cf[:], 0.0, add, mx).then_inc(sem.lb, 1)
    V.wait_ge(sem.base, 1)
    V.wait_ge(sem.mf, 1)
    V.wait_ge(sem.lb, 1)
    for s in range(N):
        V.tensor_scalar(T.t9[:, s + 1:32 * G:G], T.base[:], T.lb[:, s + 1:s + 2], T.mf[:, s:s + 1],
                        AluOpType.is_ge, mul).then_inc(sem.t9, 1)
    V.wait_ge(sem.k0, 1)
    V.wait_ge(sem.t0, 1)
    V.wait_ge(sem.t9, N)
    V.tensor_tensor_scan(T.s9[:], T.keep[:], T.t9[:], 0.0, mul, add).then_inc(sem.s9, 1)
    V.wait_ge(sem.s9, 1)
    V.tensor_scalar(T.ro[:], T.s9[:, N:32 * G:G], float(ZERO), None, mn).then_inc(sem.ro, 1)
    Y.wait_ge(sem.lb0, 1)
    Y.wait_ge(sem.lb, 1)
    Y.dma_start(T.ln[:], T.lb[0:1, 0:9]).then_inc(sem.lnst, 16)

    nc = ns = 0
    for s in others:
        gs = groups_of(topo, cores, s)
        for group in gs:
            if r in group:
                nc += len(engines_for(topo, cores, s, group, False)[r])
        for ks in SCALE_CALLS:
            both = [d for j in ks for d in gs[j]]
            if r in both:
                ns += len(engines_for(topo, cores, s, both, True)[r])
    for q in (V, A):
        q.wait_ge(sem.ro, 1)
        q.wait_ge(sem.zq, 1)
    V.wait_ge(sem.ownc, 1)
    A.wait_ge(sem.owns, 1)
    V.wait_ge(sem.arrc, nc)
    A.wait_ge(sem.arrs, ns)
    parts = [(0, PART), (PART, S_COLS)]
    for i, (a, b) in enumerate(parts):
        V.tensor_copy(T.pk[:, a:b].bitcast(dt.uint32),
                      T.land[:].bitcast(dt.uint32).indirect(T.ro[:, a // 16:b // 16])).then_inc(sem["ac%d" % i], 1)
        A.activation(T.pks[:, a:b], T.lands[:].indirect(T.ro[:, a // 16:b // 16]), copy).then_inc(sem["as%d" % i], 1)

    P.wait_ge(sem.wq, 1)
    for o in range(O):
        for i, (a, b) in enumerate(parts):
            if o == 0:
                P.wait_ge(sem["ac%d" % i], 1)
                P.wait_ge(sem["as%d" % i], 1)
            k = 2 * o + i
            P.matmul_mx(T.ps[:, 512 * k:512 * k + b - a], T.wq[:, 128 * o:128 * o + 128],
                        T.wqs[:, 128 * o:128 * o + 128], T.pk[:, a:b], T.pks[:, a:b], True,
                        True).then_inc(sem["m%d" % k], 1)
    stores = 0
    for o in range(O):
        at = S_COLS * o
        V.wait_ge(sem["m%d" % (2 * o)], 1)
        V.tensor_copy(T.yo[:, at:at + PART], T.ps[:, 1024 * o:1024 * o + PART]).then_inc(sem["yv%d" % o], 1)
        A.wait_ge(sem["m%d" % (2 * o + 1)], 1)
        A.activation(T.yo[:, at + PART:at + S_COLS], T.ps[:, 1024 * o + 512:1024 * o + 512 + S_COLS - PART],
                     copy).then_inc(sem["ys%d" % o], 1)
        cuts = [0, PART, S_COLS] if o == 0 else [0, S_COLS]
        Y.wait_ge(sem["yv%d" % o], 1)
        for a, b in zip(cuts, cuts[1:]):
            if b == S_COLS:
                Y.wait_ge(sem["ys%d" % o], 1)
            Y.dma_start(T.y[:, at + a:at + b], T.yo[:, at + a:at + b]).then_inc(sem.yst, 16)
            stores += 1

    Y.wait_ge(sem.lnst, 16)
    Y.wait_ge(sem.yst, 16 * stores)
    g.wait_ge(sem.sent, sent[0])
